import numpy as np
import ml_dtypes


def mxq(x, axis, fmt="e4m3"):
    dtype, down = {"e4m3": (ml_dtypes.float8_e4m3fn, 7), "e5m2": (ml_dtypes.float8_e5m2, 14)}[fmt]
    v = np.moveaxis(np.asarray(x, np.float32).astype(ml_dtypes.bfloat16).astype(np.float64), axis, -1)
    blocks = v.reshape(v.shape[:-1] + (-1, 32))
    amax = np.abs(blocks).max(-1, keepdims=True)
    byte = np.maximum(np.where(amax > 0, np.frexp(amax)[1] - 1 + 127, 0) - down, 1)
    scale = np.exp2(byte - 127.0)
    codes = (blocks / scale).astype(np.float32).astype(dtype).astype(np.float64)
    return np.moveaxis((codes * scale).reshape(v.shape), -1, axis)


WIDE = False


def mx_kscale(k):
    if not WIDE:
        return np.ones(k)
    levels = np.array([10, -10, 5, -5, 0])
    if k % 512:
        return np.exp2(np.random.permutation(np.resize(levels, k // 32))).repeat(32)
    a = np.empty((k // 512, 16))
    for p in range(k // 512):
        a[p, :8] = np.random.permutation(np.resize(levels, 8))
        for g in range(8):
            far = levels[np.abs(levels - a[p, g]) >= 10]
            a[p, g + 8] = far[np.random.randint(len(far))]
    return np.exp2(a.ravel()).repeat(32)


def f64(x):
    return np.asarray(x).astype(np.float64)


def striped(idx):
    return np.tile(idx.reshape(-1, 16).T, (8, 1)).astype(np.uint16)


def unstriped(offs):
    return offs[:16].T.reshape(-1).astype(np.int64)


E2M1 = np.array([0.0, 0.5, 1.0, 1.5, 2.0, 3.0, 4.0, 6.0, -0.0, -0.5, -1.0, -1.5, -2.0, -3.0, -4.0, -6.0])


def pack_weight(w, fmt):
    k, n = w.shape
    w = f64(np.asarray(w, np.float32).astype(ml_dtypes.bfloat16)).reshape(k // 32, 32, n)
    amax = np.abs(w).max(1)
    if fmt == "e4m3":
        byte = np.frexp(amax)[1] - 1 + 127 - 7
    else:
        mant, ex = np.frexp(amax / 6.0)
        byte = np.where(mant > 0.5, ex, ex - 1) + 127
    byte = np.clip(np.where(amax > 0, byte, 1), 1, 254)
    scaled = (w * np.exp2(127.0 - byte)[:, None, :]).reshape(k, n).astype(np.float32)
    by_word = np.ascontiguousarray(scaled.reshape(k // 512, 128, 4, n).transpose(0, 1, 3, 2))
    if fmt == "e4m3":
        words = by_word.astype(ml_dtypes.float8_e4m3fn).view(np.uint8)
    else:
        c = by_word.astype(ml_dtypes.float4_e2m1fn).view(np.uint8) & 0xF
        words = (c[..., 0::2] | (c[..., 1::2] << 4)).reshape(k // 512, 128, 2 * n)
    return np.ascontiguousarray(words), np.ascontiguousarray(byte.astype(np.uint8).reshape(k // 512, 16, n))


def unpack_weight(words, scales, fmt):
    g, _, n = scales.shape
    words = np.ascontiguousarray(words).reshape(g, 128, n, -1)
    if fmt == "e4m3":
        vals = words.view(ml_dtypes.float8_e4m3fn).astype(np.float64)
    else:
        nib = np.empty((g, 128, n, 4), np.uint8)
        nib[..., 0::2] = words & 0xF
        nib[..., 1::2] = words >> 4
        vals = E2M1[nib]
    vals = vals * np.repeat(np.exp2(scales.astype(np.float64) - 127.0), 8, axis=1)[..., None]
    return vals.transpose(0, 1, 3, 2).reshape(g * 512, n)


def pack_table4(v):
    words, scales = pack_weight(v, "e2m1")
    g, t = words.shape[0] // 2, v.shape[1]
    words = words.reshape(g, 2, 128, t, 2).transpose(0, 2, 3, 1, 4)
    return np.concatenate([words.reshape(g, -1), scales.reshape(g, -1)], axis=1)


def unpack_table4(tab):
    g, t = tab.shape[0], tab.shape[1] // 544
    words = tab[:, :512 * t].reshape(g, 128, t, 2, 2).transpose(0, 3, 1, 2, 4).reshape(2 * g, 128, 2 * t)
    return unpack_weight(words, tab[:, 512 * t:].reshape(2 * g, 16, t), "e2m1")


def pack_table(v):
    words, scales = pack_weight(v, "e4m3")
    return np.concatenate([words.reshape(words.shape[0], -1), scales.reshape(scales.shape[0], -1)], axis=1)


def unpack_table(tab):
    g, t = tab.shape[0], tab.shape[1] // 528
    return unpack_weight(tab[:, :512 * t].reshape(g, 128, t, 4), tab[:, 512 * t:].reshape(g, 16, t), "e4m3")


K, L, M, T, S = 1536, 2048, 512, 4096, 2048


def setup_inputs():
    n = np.random.standard_normal
    s1 = mx_kscale(K)[:, None]
    s2 = mx_kscale(L)[:, None]
    p_w4 = pack_weight(n((K, M)) / np.sqrt(K) / s1, "e2m1")
    return {
        "tab": pack_table(n((K, T)) * s1),
        "w4_words": p_w4[0],
        "w4_scales": p_w4[1],
        "tab2": pack_table4(n((L, T)) * s2),
        "u": (n((L, M)) / np.sqrt(L) / s2).astype(np.float32),
        "r": (n((512, 2048))).astype(np.float32),
        "offs": striped(np.random.permutation(T)[:S]),
        "offs2": striped(np.random.permutation(T)[:S]),
    }


def reference(tab, w4_words, w4_scales, tab2, u, r, offs, offs2):
    tab_ = unpack_table(tab)[:, unstriped(offs)]
    w4_ = unpack_weight(w4_words, w4_scales, "e2m1")
    tab2_ = unpack_table4(tab2)[:, unstriped(offs2)]
    u_ = mxq(f64(u), 0, "e4m3")
    y = w4_.T @ tab_ + u_.T @ tab2_
    return f64(r) + y

@@ -1,0 +1,268 @@
+from contextlib import ExitStack
+
+import concourse.mybir as mybir
+
+K, L, M, T, S = 1536, 2048, 512, 4096, 2048
+P = 128
+TAB_PASSES = K // 512
+U_PASSES = L // 512
+N = 512
+HALF = S // 2
+FLOPS = 2 * (K + L) * M * S
+
+F32 = mybir.dt.float32
+BF16 = mybir.dt.bfloat16
+I32 = mybir.dt.int32
+U32 = mybir.dt.uint32
+U16 = mybir.dt.uint16
+U8 = mybir.dt.uint8
+FP8X4 = mybir.dt.float8_e4m3fn_x4
+FP4X4 = mybir.dt.float4_e2m1fn_x4
+ADD = mybir.AluOpType.add
+
+
+def tile_list_tab48_res_kernel(tc, tab, w4_words, w4_scales, tab2, u, r, offs, offs2, out):
+    nc = tc.nc
+    with ExitStack() as ctx:
+        keep = ctx.enter_context(tc.tile_pool(name="keep", bufs=1))
+        stage = ctx.enter_context(tc.tile_pool(name="stage", bufs=2))
+        swap = ctx.enter_context(tc.tile_pool(name="swap", bufs=2))
+        ring = ctx.enter_context(tc.tile_pool(name="ring", bufs=8))
+        psum = ctx.enter_context(tc.psum_pool(name="psum", bufs=1))
+
+        offs_t = keep.tile([P, S // 16], U16, name="offs_t")
+        offs2_t = keep.tile([P, S // 16], U16, name="offs2_t")
+        nc.sync.dma_start(offs_t[:], offs)
+
+        tab_w = [keep.tile([P, T], I32, name=f"tab_w{a}", align_bytes=64) for a in range(TAB_PASSES)]
+        tab_s = [keep.tile([P, T // 4], I32, name=f"tab_s{a}", align_bytes=64) for a in range(TAB_PASSES)]
+        tab2_w = [keep.tile([P, T], I32, name=f"tab2_w{m}", align_bytes=64) for m in range(2)]
+        tab2_s = keep.tile([P, T // 4], I32, name="tab2_s", align_bytes=64)
+        w4_w = keep.tile([P, TAB_PASSES, M // 2], I32, name="w4_w", align_bytes=64)
+        w4_s = keep.tile([P, TAB_PASSES, M // 4], I32, name="w4_s", align_bytes=64)
+
+        nc.vector.memset(tab_s[1][:], 0)
+        nc.gpsimd.memset(tab2_s[:], 0)
+        nc.vector.memset(w4_s[:], 0)
+        nc.vector.memset(tab_s[2][:], 0)
+
+        def load_tab_words(a):
+            nc.sync.dma_start(tab_w[a][:], tab[a, 0 : 512 * T].rearrange("(p b) -> p b", p=P).bitcast(I32))
+
+        def load_tab_scales_wide(a):
+            flat = tab.rearrange("a b -> (a b)")
+            for q in range(4):
+                at = a * 528 * T + (512 + 4 * q) * T
+                rows = flat[at : at + 32 * T].rearrange("(p b) -> p b", p=32).bitcast(I32)
+                nc.sync.dma_start(tab_s[a][32 * q : 32 * (q + 1), :], rows)
+
+        def load_tab_scales(a, queue):
+            rows = tab[a, 512 * T : 528 * T].rearrange("(q b) -> q b", q=16).bitcast(I32)
+            for q in range(4):
+                queue.dma_start(tab_s[a][32 * q : 32 * q + 4, :], rows[4 * q : 4 * q + 4, :])
+
+        def load_tab2_words(m):
+            nc.sync.dma_start(tab2_w[m][:], tab2[m, 0 : 512 * T].rearrange("(p b) -> p b", p=P).bitcast(I32))
+
+        def load_tab2_scales():
+            for m in range(2):
+                rows = tab2[m, 512 * T : 544 * T].rearrange("(h q b) -> h q b", h=2, q=16).bitcast(I32)
+                for q in range(4):
+                    lo = 32 * q + 8 * m
+                    nc.gpsimd.dma_start(tab2_s[lo : lo + 8, :], rows[:, 4 * q : 4 * q + 4, :])
+
+        def load_w4():
+            nc.scalar.dma_start(w4_w[:], w4_words.rearrange("a p b -> p a b").bitcast(I32))
+            for q in range(4):
+                rows = w4_scales[:, 4 * q : 4 * q + 4, :].rearrange("a r b -> r a b").bitcast(I32)
+                nc.scalar.dma_start(w4_s[32 * q : 32 * q + 4, :, :], rows)
+
+        u_raw = {}
+
+        def load_u(a):
+            if a % 2 == 0:
+                pair = swap.tile([P, 2, 4, M], F32, name="pair_u", tag="swap")
+                u_raw[a] = pair[:, 0, :, :]
+                u_raw[a + 1] = pair[:, 1, :, :]
+            nc.sync.dma_start(u_raw[a], u[512 * a : 512 * (a + 1), :].rearrange("(p j) n -> p j n", j=4))
+
+        r_t = {}
+
+        def load_r(h):
+            r_t[h] = swap.tile([P, 4, HALF], F32, name="r_half", tag="swap")
+            nc.sync.dma_start(r_t[h][:], r[:, HALF * h : HALF * (h + 1)].rearrange("(m p) j -> p m j", p=P))
+
+        load_tab_scales_wide(0)
+        load_tab_words(0)
+        load_tab_scales(1, nc.scalar)
+        load_tab_words(1)
+        nc.sync.dma_start(offs2_t[:], offs2)
+        load_tab2_scales()
+        load_w4()
+        load_tab2_words(0)
+        load_u(0)
+        load_u(1)
+        load_tab_scales(2, nc.gpsimd)
+        load_tab2_words(1)
+        load_u(2)
+        load_u(3)
+        load_tab_words(2)
+
+        def cols(lo, n):
+            return slice(lo // 16, (lo + n) // 16)
+
+        gs = {}
+        gw = {}
+        g2s = {}
+        g2w = {}
+
+        def gather_tab_scales(a, lo, n):
+            t = keep.tile([P, n // 4], I32, name=f"gs{a}_{lo}", align_bytes=64)
+            nc.vector.tensor_copy(t[:].bitcast(U8), tab_s[a][:].bitcast(U8).indirect(offs_t[:, cols(lo, n)]))
+            for c in range(lo, lo + n, N):
+                gs[a, c // N] = t[:].bitcast(U8)[:, c - lo : c - lo + N]
+
+        def gather_tab_words(a, lo, n):
+            t = keep.tile([P, n], I32, name=f"gw{a}_{lo}", align_bytes=64)
+            nc.vector.tensor_copy(t[:].bitcast(U32), tab_w[a][:].bitcast(U32).indirect(offs_t[:, cols(lo, n)]))
+            for c in range(lo, lo + n, N):
+                gw[a, c // N] = t[:, c - lo : c - lo + N].bitcast(FP8X4)
+
+        def gather_tab2_scales(lo, n):
+            packed = keep.tile([P, n // 4], I32, name=f"g2s_{lo}", align_bytes=64)
+            nc.vector.tensor_copy(packed[:].bitcast(U8), tab2_s[:].bitcast(U8).indirect(offs2_t[:, cols(lo, n)]))
+            for b in range(U_PASSES):
+                if b == 0:
+                    t = packed
+                else:
+                    t = moved[b, lo]
+                    nc.gpsimd.dma_start(t[0:112, :], packed[4 * b : 4 * b + 112, :])
+                for c in range(lo, lo + n, N):
+                    g2s[b, c // N] = t[:].bitcast(U8)[:, c - lo : c - lo + N]
+
+        def gather_tab2_words(m, lo, n):
+            t = stage.tile([P, HALF], I32, name="pair")
+            nc.vector.tensor_copy(t[:, 0:n].bitcast(U32), tab2_w[m][:].bitcast(U32).indirect(offs2_t[:, cols(lo, n)]))
+            w = keep.tile([P, 2, 2 * n], U8, name=f"g2w{m}_{lo}", align_bytes=64)
+            nc.vector.tensor_copy(w[:].bitcast(U16), t[:, 0:n].bitcast(U16).rearrange("p (n h) -> p h n", h=2))
+            for h in range(2):
+                for c in range(lo, lo + n, N):
+                    g2w[2 * m + h, c // N] = w[:, h, 2 * (c - lo) : 2 * (c - lo + N)].bitcast(FP4X4)
+
+        moved = {}
+        for b in range(1, U_PASSES):
+            for lo in (0, HALF):
+                moved[b, lo] = keep.tile([P, HALF // 4], I32, name=f"moved{b}_{lo}", align_bytes=64)
+                nc.gpsimd.memset(moved[b, lo][:], 0)
+
+        u_codes = {}
+        u_scales = {}
+
+        def interleave_u(a):
+            grouped = stage.tile([P, M, 4], BF16, name="grouped", align_bytes=64)
+            nc.scalar.copy(grouped[:], u_raw[a].rearrange("p j n -> p n j"))
+            u_codes[a] = keep.tile([P, M], U32, name=f"u_codes{a}", align_bytes=64)
+            u_scales[a] = keep.tile([P, M], U8, name=f"u_scales{a}", align_bytes=64)
+            return grouped
+
+        def quantise_u(a, grouped):
+            nc.vector.quantize_mx(
+                out=u_codes[a][:].bitcast(FP8X4), scales=u_scales[a][:], in_=grouped[:].rearrange("p n j -> p (n j)")
+            )
+
+        acc = {}
+
+        def banks(c):
+            for m in range(4):
+                acc[c, m] = psum.tile([P, N], F32, name=f"bank{c % 2}{m}")
+
+        def multiply_tab(a, c, start, stop):
+            for m in range(4):
+                nc.tensor.matmul_mx(
+                    out=acc[c, m][:],
+                    lhsT=w4_w[:, a, 64 * m : 64 * (m + 1)].bitcast(FP4X4),
+                    lhsT_scale=w4_s[:, a, 32 * m : 32 * (m + 1)].bitcast(U8),
+                    rhs=gw[a, c],
+                    rhs_scale=gs[a, c],
+                    start=start,
+                    stop=stop,
+                )
+
+        def multiply_tab2(b, c, start, stop):
+            for m in range(4):
+                nc.tensor.matmul_mx(
+                    out=acc[c, m][:],
+                    lhsT=u_codes[b][:, P * m : P * (m + 1)].bitcast(FP8X4),
+                    lhsT_scale=u_scales[b][:, P * m : P * (m + 1)],
+                    rhs=g2w[b, c],
+                    rhs_scale=g2s[b, c],
+                    start=start,
+                    stop=stop,
+                )
+
+        def finish(c, m, on_vector):
+            res = r_t[c // 2][:, m, N * (c % 2) : N * (c % 2 + 1)]
+            o = ring.tile([P, N], F32, name="o")
+            if on_vector:
+                nc.vector.tensor_tensor(o[:], acc[c, m][:], res, ADD)
+            else:
+                nc.scalar.copy(o[:], acc[c, m][:])
+                nc.gpsimd.tensor_tensor(o[:], o[:], res, ADD)
+            nc.sync.dma_start(out[P * m : P * (m + 1), N * c : N * (c + 1)], o[:])
+
+        banks(0)
+        banks(1)
+        gather_tab_scales(0, 0, S)
+        gather_tab_words(0, 0, HALF)
+        for c in (0, 1):
+            multiply_tab(0, c, True, False)
+        gather_tab_scales(1, 0, HALF)
+        gather_tab_words(1, 0, HALF)
+        for c in (0, 1):
+            multiply_tab(1, c, False, False)
+        gather_tab_words(0, HALF, HALF)
+        g0 = interleave_u(0)
+        g1 = interleave_u(1)
+        gather_tab2_scales(0, HALF)
+        gather_tab2_words(0, 0, HALF)
+        gather_tab_scales(1, HALF, HALF)
+        quantise_u(0, g0)
+        quantise_u(1, g1)
+        for b in (0, 1):
+            for c in (0, 1):
+                multiply_tab2(b, c, False, False)
+        load_r(0)
+        g2 = interleave_u(2)
+        g3 = interleave_u(3)
+        load_r(1)
+        gather_tab2_words(1, 0, HALF)
+        gather_tab_scales(2, 0, HALF)
+        quantise_u(2, g2)
+        quantise_u(3, g3)
+        for b in (2, 3):
+            for c in (0, 1):
+                multiply_tab2(b, c, False, False)
+        for c in (0, 1):
+            gather_tab_words(2, N * c, N)
+            multiply_tab(2, c, False, True)
+            for m in range(4):
+                finish(c, m, False)
+
+        gather_tab2_scales(HALF, HALF)
+        gather_tab_words(1, HALF, HALF)
+        for c in (2, 3):
+            banks(c)
+            multiply_tab(0, c, True, False)
+            multiply_tab(1, c, False, False)
+        for c in (2, 3):
+            lo = N * c
+            for h in (0, 1):
+                gather_tab2_words(h, lo, N)
+                for b in (2 * h, 2 * h + 1):
+                    multiply_tab2(b, c, False, False)
+            if c == 2:
+                gather_tab_scales(2, HALF, HALF)
+            gather_tab_words(2, lo, N)
+            multiply_tab(2, c, False, True)
+            for m in range(4):
+                finish(c, m, c == 3 and m > 0)

@@ -32,81 +32,84 @@ def tile_list_tab48_res_kernel(tc, tab, w4_words, w4_scales, tab2, u, r, offs, o
 
         offs_t = keep.tile([P, S // 16], U16, name="offs_t")
         offs2_t = keep.tile([P, S // 16], U16, name="offs2_t")
-        nc.sync.dma_start(offs_t[:], offs)
-
-        tab_w = [keep.tile([P, T], I32, name=f"tab_w{a}", align_bytes=64) for a in range(TAB_PASSES)]
-        tab_s = [keep.tile([P, T // 4], I32, name=f"tab_s{a}", align_bytes=64) for a in range(TAB_PASSES)]
-        tab2_w = [keep.tile([P, T], I32, name=f"tab2_w{m}", align_bytes=64) for m in range(2)]
+        tab_s0 = keep.tile([P, T // 4], I32, name="tab_s0", align_bytes=64)
+        tab_s12 = keep.tile([P, 2, T // 4], I32, name="tab_s12", align_bytes=64)
+        tab_s = [tab_s0[:], tab_s12[:, 0, :], tab_s12[:, 1, :]]
         tab2_s = keep.tile([P, T // 4], I32, name="tab2_s", align_bytes=64)
+        tab_w = [keep.tile([P, T], I32, name=f"tab_w{a}", align_bytes=64) for a in range(2)]
+        tab2_w = [keep.tile([P, T], I32, name=f"tab2_w{m}", align_bytes=64) for m in range(2)]
         w4_w = keep.tile([P, TAB_PASSES, M // 2], I32, name="w4_w", align_bytes=64)
         w4_s = keep.tile([P, TAB_PASSES, M // 4], I32, name="w4_s", align_bytes=64)
-
-        nc.vector.memset(tab_s[1][:], 0)
-        nc.gpsimd.memset(tab2_s[:], 0)
-        nc.vector.memset(w4_s[:], 0)
-        nc.vector.memset(tab_s[2][:], 0)
+        moved = [keep.tile([P, S // 4], I32, name=f"moved{b}", align_bytes=64) for b in range(1, U_PASSES)]
+        u_raw = {}
+        r_t = {}
 
         def load_tab_words(a):
+            if a == 2:
+                tab_w.append(keep.tile([P, T], I32, name="tab_w2", tag="tab_w1", align_bytes=64))
             nc.sync.dma_start(tab_w[a][:], tab[a, 0 : 512 * T].rearrange("(p b) -> p b", p=P).bitcast(I32))
-
-        def load_tab_scales_wide(a):
-            flat = tab.rearrange("a b -> (a b)")
-            for q in range(4):
-                at = a * 528 * T + (512 + 4 * q) * T
-                rows = flat[at : at + 32 * T].rearrange("(p b) -> p b", p=32).bitcast(I32)
-                nc.sync.dma_start(tab_s[a][32 * q : 32 * (q + 1), :], rows)
-
-        def load_tab_scales(a, queue):
-            rows = tab[a, 512 * T : 528 * T].rearrange("(q b) -> q b", q=16).bitcast(I32)
-            for q in range(4):
-                queue.dma_start(tab_s[a][32 * q : 32 * q + 4, :], rows[4 * q : 4 * q + 4, :])
 
         def load_tab2_words(m):
             nc.sync.dma_start(tab2_w[m][:], tab2[m, 0 : 512 * T].rearrange("(p b) -> p b", p=P).bitcast(I32))
-
-        def load_tab2_scales():
-            for m in range(2):
-                rows = tab2[m, 512 * T : 544 * T].rearrange("(h q b) -> h q b", h=2, q=16).bitcast(I32)
-                for q in range(4):
-                    lo = 32 * q + 8 * m
-                    nc.gpsimd.dma_start(tab2_s[lo : lo + 8, :], rows[:, 4 * q : 4 * q + 4, :])
-
-        def load_w4():
-            nc.scalar.dma_start(w4_w[:], w4_words.rearrange("a p b -> p a b").bitcast(I32))
-            for q in range(4):
-                rows = w4_scales[:, 4 * q : 4 * q + 4, :].rearrange("a r b -> r a b").bitcast(I32)
-                nc.scalar.dma_start(w4_s[32 * q : 32 * q + 4, :, :], rows)
-
-        u_raw = {}
 
         def load_u(a):
             if a % 2 == 0:
                 pair = swap.tile([P, 2, 4, M], F32, name="pair_u", tag="swap")
                 u_raw[a] = pair[:, 0, :, :]
                 u_raw[a + 1] = pair[:, 1, :, :]
+            hold(u_raw[a][:, 0, 0:16])
             nc.sync.dma_start(u_raw[a], u[512 * a : 512 * (a + 1), :].rearrange("(p j) n -> p j n", j=4))
-
-        r_t = {}
 
         def load_r(h):
             r_t[h] = swap.tile([P, 4, HALF], F32, name="r_half", tag="swap")
             nc.sync.dma_start(r_t[h][:], r[:, HALF * h : HALF * (h + 1)].rearrange("(m p) j -> p m j", p=P))
 
-        load_tab_scales_wide(0)
-        load_tab_words(0)
-        load_tab_scales(1, nc.scalar)
-        load_tab_words(1)
+        tab2_rows = tab2[:, 512 * T : 544 * T].rearrange("m (h q b) -> m h q b", h=2, q=16).bitcast(I32)
+
+        def hold(view):
+            nc.vector.memset(view, 0)
+        tab_rows = tab[1:3, 512 * T : 528 * T].rearrange("a (q b) -> q a b", q=16).bitcast(I32)
+        flat = tab.rearrange("a b -> (a b)")
+
+        def load_tab2_scales(m, q):
+            lo = 32 * q + 8 * m
+            nc.scalar.dma_start(tab2_s[lo : lo + 8, :], tab2_rows[m, :, 4 * q : 4 * q + 4, :])
+
+        def load_tab_scales(q):
+            nc.scalar.dma_start(tab_s12[32 * q : 32 * q + 4, :, :], tab_rows[4 * q : 4 * q + 4, :, :])
+
+        nc.vector.memset(tab2_s[:], 0)
+        nc.gpsimd.memset(w4_s[:], 0)
+        nc.sync.dma_start(offs_t[:], offs)
         nc.sync.dma_start(offs2_t[:], offs2)
-        load_tab2_scales()
-        load_w4()
+        for q in range(4):
+            rows = flat[(512 + 4 * q) * T : (544 + 4 * q) * T].rearrange("(p b) -> p b", p=32).bitcast(I32)
+            nc.sync.dma_start(tab_s0[32 * q : 32 * (q + 1), :], rows)
+        load_tab_words(0)
+        nc.gpsimd.dma_start(w4_w[:], w4_words.rearrange("a p b -> p a b").bitcast(I32))
+        for q in range(4):
+            rows = w4_scales[:, 4 * q : 4 * q + 4, :].rearrange("a r b -> r a b").bitcast(I32)
+            nc.gpsimd.dma_start(w4_s[32 * q : 32 * q + 4, :, :], rows)
+        for m in range(2):
+            for q in range(4):
+                load_tab2_scales(m, q)
+        nc.vector.memset(moved[0][:, 0:256], 0)
+        hold(tab_w[1][:, 0:16])
+        load_tab_words(1)
+        nc.vector.memset(tab_s12[:], 0)
+        for q in range(4):
+            load_tab_scales(q)
+        hold(tab2_w[0][:, 0:16])
         load_tab2_words(0)
         load_u(0)
         load_u(1)
-        load_tab_scales(2, nc.gpsimd)
+        hold(tab2_w[1][:, 0:16])
         load_tab2_words(1)
         load_u(2)
         load_u(3)
-        load_tab_words(2)
+        nc.gpsimd.memset(moved[0][:, 256:512], 0)
+        for b in range(2, U_PASSES):
+            nc.gpsimd.memset(moved[b - 1][:], 0)
 
         def cols(lo, n):
             return slice(lo // 16, (lo + n) // 16)
@@ -114,46 +117,51 @@ def tile_list_tab48_res_kernel(tc, tab, w4_words, w4_scales, tab2, u, r, offs, o
         gs = {}
         gw = {}
         g2s = {}
+        second_scales = []
         g2w = {}
 
         def gather_tab_scales(a, lo, n):
-            t = keep.tile([P, n // 4], I32, name=f"gs{a}_{lo}", align_bytes=64)
-            nc.vector.tensor_copy(t[:].bitcast(U8), tab_s[a][:].bitcast(U8).indirect(offs_t[:, cols(lo, n)]))
+            if lo == HALF:
+                if a == 1:
+                    second_scales.append(keep.tile([P, 2, HALF // 4], I32, name="gs_b", tag="late0", align_bytes=64))
+                t = second_scales[0][:, a - 1, :]
+            else:
+                whole = keep.tile([P, n // 4], I32, name=f"gs{a}_{lo}", align_bytes=64)
+                t = whole[:]
+            nc.vector.tensor_copy(t.bitcast(U8), tab_s[a].bitcast(U8).indirect(offs_t[:, cols(lo, n)]))
             for c in range(lo, lo + n, N):
-                gs[a, c // N] = t[:].bitcast(U8)[:, c - lo : c - lo + N]
+                gs[a, c // N] = t.bitcast(U8)[:, c - lo : c - lo + N]
 
         def gather_tab_words(a, lo, n):
-            t = keep.tile([P, n], I32, name=f"gw{a}_{lo}", align_bytes=64)
+            if a == 2 and lo < HALF:
+                t = keep.tile([P, n], I32, name=f"gw{a}_{lo}", tag=f"late{lo // N}", align_bytes=64)
+            else:
+                t = keep.tile([P, n], I32, name=f"gw{a}_{lo}", align_bytes=64)
             nc.vector.tensor_copy(t[:].bitcast(U32), tab_w[a][:].bitcast(U32).indirect(offs_t[:, cols(lo, n)]))
             for c in range(lo, lo + n, N):
                 gw[a, c // N] = t[:, c - lo : c - lo + N].bitcast(FP8X4)
 
-        def gather_tab2_scales(lo, n):
-            packed = keep.tile([P, n // 4], I32, name=f"g2s_{lo}", align_bytes=64)
-            nc.vector.tensor_copy(packed[:].bitcast(U8), tab2_s[:].bitcast(U8).indirect(offs2_t[:, cols(lo, n)]))
+        def gather_tab2_scales():
+            packed = keep.tile([P, S // 4], I32, name="g2s", align_bytes=64)
+            nc.vector.tensor_copy(packed[:].bitcast(U8), tab2_s[:].bitcast(U8).indirect(offs2_t[:]))
             for b in range(U_PASSES):
-                if b == 0:
-                    t = packed
-                else:
-                    t = moved[b, lo]
-                    nc.gpsimd.dma_start(t[0:112, :], packed[4 * b : 4 * b + 112, :])
-                for c in range(lo, lo + n, N):
-                    g2s[b, c // N] = t[:].bitcast(U8)[:, c - lo : c - lo + N]
+                t = packed if b == 0 else moved[b - 1]
+                if b > 0:
+                    nc.scalar.dma_start(t[0:112, :], packed[4 * b : 4 * b + 112, :])
+                for c in range(S // N):
+                    g2s[b, c] = t[:].bitcast(U8)[:, N * c : N * (c + 1)]
 
         def gather_tab2_words(m, lo, n):
-            t = stage.tile([P, HALF], I32, name="pair")
+            if lo == 0:
+                t = keep.tile([P, HALF], I32, name=f"pair{m}", align_bytes=64)
+            else:
+                t = keep.tile([P, N], I32, name=f"pair{m}_{lo}", tag="late1", align_bytes=64)
             nc.vector.tensor_copy(t[:, 0:n].bitcast(U32), tab2_w[m][:].bitcast(U32).indirect(offs2_t[:, cols(lo, n)]))
             w = keep.tile([P, 2, 2 * n], U8, name=f"g2w{m}_{lo}", align_bytes=64)
             nc.vector.tensor_copy(w[:].bitcast(U16), t[:, 0:n].bitcast(U16).rearrange("p (n h) -> p h n", h=2))
             for h in range(2):
                 for c in range(lo, lo + n, N):
                     g2w[2 * m + h, c // N] = w[:, h, 2 * (c - lo) : 2 * (c - lo + N)].bitcast(FP4X4)
-
-        moved = {}
-        for b in range(1, U_PASSES):
-            for lo in (0, HALF):
-                moved[b, lo] = keep.tile([P, HALF // 4], I32, name=f"moved{b}_{lo}", align_bytes=64)
-                nc.gpsimd.memset(moved[b, lo][:], 0)
 
         u_codes = {}
         u_scales = {}
@@ -216,16 +224,17 @@ def tile_list_tab48_res_kernel(tc, tab, w4_words, w4_scales, tab2, u, r, offs, o
         gather_tab_words(0, 0, HALF)
         for c in (0, 1):
             multiply_tab(0, c, True, False)
-        gather_tab_scales(1, 0, HALF)
+        gather_tab_words(0, HALF, HALF)
+        gather_tab2_scales()
         gather_tab_words(1, 0, HALF)
+        gather_tab_words(1, HALF, HALF)
+        load_tab_words(2)
+        gather_tab_scales(1, 0, HALF)
         for c in (0, 1):
             multiply_tab(1, c, False, False)
-        gather_tab_words(0, HALF, HALF)
         g0 = interleave_u(0)
         g1 = interleave_u(1)
-        gather_tab2_scales(0, HALF)
         gather_tab2_words(0, 0, HALF)
-        gather_tab_scales(1, HALF, HALF)
         quantise_u(0, g0)
         quantise_u(1, g1)
         for b in (0, 1):
@@ -248,8 +257,8 @@ def tile_list_tab48_res_kernel(tc, tab, w4_words, w4_scales, tab2, u, r, offs, o
             for m in range(4):
                 finish(c, m, False)
 
-        gather_tab2_scales(HALF, HALF)
-        gather_tab_words(1, HALF, HALF)
+        gather_tab_scales(1, HALF, HALF)
+        gather_tab_scales(2, HALF, HALF)
         for c in (2, 3):
             banks(c)
             multiply_tab(0, c, True, False)
@@ -260,8 +269,6 @@ def tile_list_tab48_res_kernel(tc, tab, w4_words, w4_scales, tab2, u, r, offs, o
                 gather_tab2_words(h, lo, N)
                 for b in (2 * h, 2 * h + 1):
                     multiply_tab2(b, c, False, False)
-            if c == 2:
-                gather_tab_scales(2, HALF, HALF)
             gather_tab_words(2, lo, N)
             multiply_tab(2, c, False, True)
             for m in range(4):

@@ -208,15 +208,23 @@ def tile_list_tab48_res_kernel(tc, tab, w4_words, w4_scales, tab2, u, r, offs, o
                     stop=stop,
                 )
 
-        def finish(c, m, on_vector):
-            res = r_t[c // 2][:, m, N * (c % 2) : N * (c % 2 + 1)]
-            o = ring.tile([P, N], F32, name="o")
-            if on_vector:
-                nc.vector.tensor_tensor(o[:], acc[c, m][:], res, ADD)
-            else:
-                nc.scalar.copy(o[:], acc[c, m][:])
-                nc.gpsimd.tensor_tensor(o[:], o[:], res, ADD)
-            nc.sync.dma_start(out[P * m : P * (m + 1), N * c : N * (c + 1)], o[:])
+        copied = {}
+
+        def empty_banks(c):
+            for m in range(4):
+                copied[c, m] = ring.tile([P, N], F32, name="o")
+                nc.scalar.copy(copied[c, m][:], acc[c, m][:])
+
+        def add_and_store(c):
+            for m in range(4):
+                res = r_t[c // 2][:, m, N * (c % 2) : N * (c % 2 + 1)]
+                if (c, m) in copied:
+                    o = copied[c, m]
+                    nc.vector.tensor_tensor(o[:], o[:], res, ADD)
+                else:
+                    o = ring.tile([P, N], F32, name="o")
+                    nc.vector.tensor_tensor(o[:], acc[c, m][:], res, ADD)
+                nc.sync.dma_start(out[P * m : P * (m + 1), N * c : N * (c + 1)], o[:])
 
         banks(0)
         banks(1)
@@ -254,8 +262,7 @@ def tile_list_tab48_res_kernel(tc, tab, w4_words, w4_scales, tab2, u, r, offs, o
         for c in (0, 1):
             gather_tab_words(2, N * c, N)
             multiply_tab(2, c, False, True)
-            for m in range(4):
-                finish(c, m, False)
+            empty_banks(c)
 
         gather_tab_scales(1, HALF, HALF)
         gather_tab_scales(2, HALF, HALF)
@@ -271,5 +278,6 @@ def tile_list_tab48_res_kernel(tc, tab, w4_words, w4_scales, tab2, u, r, offs, o
                     multiply_tab2(b, c, False, False)
             gather_tab_words(2, lo, N)
             multiply_tab(2, c, False, True)
-            for m in range(4):
-                finish(c, m, c == 3 and m > 0)
+            add_and_store(c - 2)
+        add_and_store(2)
+        add_and_store(3)

from contextlib import ExitStack

import concourse.mybir as mybir

K, L, M, T, S = 1536, 2048, 512, 4096, 2048
P = 128
TAB_PASSES = K // 512
U_PASSES = L // 512
N = 512
HALF = S // 2
FLOPS = 2 * (K + L) * M * S

F32 = mybir.dt.float32
BF16 = mybir.dt.bfloat16
I32 = mybir.dt.int32
U32 = mybir.dt.uint32
U16 = mybir.dt.uint16
U8 = mybir.dt.uint8
FP8X4 = mybir.dt.float8_e4m3fn_x4
FP4X4 = mybir.dt.float4_e2m1fn_x4
ADD = mybir.AluOpType.add


def tile_list_tab48_res_kernel(tc, tab, w4_words, w4_scales, tab2, u, r, offs, offs2, out):
    nc = tc.nc
    with ExitStack() as ctx:
        keep = ctx.enter_context(tc.tile_pool(name="keep", bufs=1))
        stage = ctx.enter_context(tc.tile_pool(name="stage", bufs=2))
        swap = ctx.enter_context(tc.tile_pool(name="swap", bufs=2))
        ring = ctx.enter_context(tc.tile_pool(name="ring", bufs=8))
        psum = ctx.enter_context(tc.psum_pool(name="psum", bufs=1))

        offs_t = keep.tile([P, S // 16], U16, name="offs_t")
        offs2_t = keep.tile([P, S // 16], U16, name="offs2_t")
        tab_s0 = keep.tile([P, T // 4], I32, name="tab_s0", align_bytes=64)
        tab_s12 = keep.tile([P, 2, T // 4], I32, name="tab_s12", align_bytes=64)
        tab_s = [tab_s0[:], tab_s12[:, 0, :], tab_s12[:, 1, :]]
        tab2_s = keep.tile([P, T // 4], I32, name="tab2_s", align_bytes=64)
        tab_w = [keep.tile([P, T], I32, name=f"tab_w{a}", align_bytes=64) for a in range(2)]
        tab2_w = [keep.tile([P, T], I32, name=f"tab2_w{m}", align_bytes=64) for m in range(2)]
        w4_w = keep.tile([P, TAB_PASSES, M // 2], I32, name="w4_w", align_bytes=64)
        w4_s = keep.tile([P, TAB_PASSES, M // 4], I32, name="w4_s", align_bytes=64)
        moved = [keep.tile([P, S // 4], I32, name=f"moved{b}", align_bytes=64) for b in range(1, U_PASSES)]
        u_raw = {}
        r_t = {}

        def load_tab_words(a):
            if a == 2:
                tab_w.append(keep.tile([P, T], I32, name="tab_w2", tag="tab_w1", align_bytes=64))
            nc.sync.dma_start(tab_w[a][:], tab[a, 0 : 512 * T].rearrange("(p b) -> p b", p=P).bitcast(I32))

        def load_tab2_words(m):
            nc.sync.dma_start(tab2_w[m][:], tab2[m, 0 : 512 * T].rearrange("(p b) -> p b", p=P).bitcast(I32))

        def load_u(a):
            if a % 2 == 0:
                pair = swap.tile([P, 2, 4, M], F32, name="pair_u", tag="swap")
                u_raw[a] = pair[:, 0, :, :]
                u_raw[a + 1] = pair[:, 1, :, :]
            hold(u_raw[a][:, 0, 0:16])
            nc.sync.dma_start(u_raw[a], u[512 * a : 512 * (a + 1), :].rearrange("(p j) n -> p j n", j=4))

        def load_r(h):
            r_t[h] = swap.tile([P, 4, HALF], F32, name="r_half", tag="swap")
            nc.sync.dma_start(r_t[h][:], r[:, HALF * h : HALF * (h + 1)].rearrange("(m p) j -> p m j", p=P))

        tab2_rows = tab2[:, 512 * T : 544 * T].rearrange("m (h q b) -> m h q b", h=2, q=16).bitcast(I32)

        def hold(view):
            nc.vector.memset(view, 0)
        tab_rows = tab[1:3, 512 * T : 528 * T].rearrange("a (q b) -> q a b", q=16).bitcast(I32)
        flat = tab.rearrange("a b -> (a b)")

        def load_tab2_scales(m, q):
            lo = 32 * q + 8 * m
            nc.scalar.dma_start(tab2_s[lo : lo + 8, :], tab2_rows[m, :, 4 * q : 4 * q + 4, :])

        def load_tab_scales(q):
            nc.scalar.dma_start(tab_s12[32 * q : 32 * q + 4, :, :], tab_rows[4 * q : 4 * q + 4, :, :])

        nc.vector.memset(tab2_s[:], 0)
        nc.gpsimd.memset(w4_s[:], 0)
        nc.sync.dma_start(offs_t[:], offs)
        nc.sync.dma_start(offs2_t[:], offs2)
        for q in range(4):
            rows = flat[(512 + 4 * q) * T : (544 + 4 * q) * T].rearrange("(p b) -> p b", p=32).bitcast(I32)
            nc.sync.dma_start(tab_s0[32 * q : 32 * (q + 1), :], rows)
        load_tab_words(0)
        nc.gpsimd.dma_start(w4_w[:], w4_words.rearrange("a p b -> p a b").bitcast(I32))
        for q in range(4):
            rows = w4_scales[:, 4 * q : 4 * q + 4, :].rearrange("a r b -> r a b").bitcast(I32)
            nc.gpsimd.dma_start(w4_s[32 * q : 32 * q + 4, :, :], rows)
        for m in range(2):
            for q in range(4):
                load_tab2_scales(m, q)
        nc.vector.memset(moved[0][:, 0:256], 0)
        hold(tab_w[1][:, 0:16])
        load_tab_words(1)
        nc.vector.memset(tab_s12[:], 0)
        for q in range(4):
            load_tab_scales(q)
        hold(tab2_w[0][:, 0:16])
        load_tab2_words(0)
        load_u(0)
        load_u(1)
        hold(tab2_w[1][:, 0:16])
        load_tab2_words(1)
        load_u(2)
        load_u(3)
        nc.gpsimd.memset(moved[0][:, 256:512], 0)
        for b in range(2, U_PASSES):
            nc.gpsimd.memset(moved[b - 1][:], 0)

        def cols(lo, n):
            return slice(lo // 16, (lo + n) // 16)

        gs = {}
        gw = {}
        g2s = {}
        second_scales = []
        g2w = {}

        def gather_tab_scales(a, lo, n):
            if lo == HALF:
                if a == 1:
                    second_scales.append(keep.tile([P, 2, HALF // 4], I32, name="gs_b", tag="late0", align_bytes=64))
                t = second_scales[0][:, a - 1, :]
            else:
                whole = keep.tile([P, n // 4], I32, name=f"gs{a}_{lo}", align_bytes=64)
                t = whole[:]
            nc.vector.tensor_copy(t.bitcast(U8), tab_s[a].bitcast(U8).indirect(offs_t[:, cols(lo, n)]))
            for c in range(lo, lo + n, N):
                gs[a, c // N] = t.bitcast(U8)[:, c - lo : c - lo + N]

        def gather_tab_words(a, lo, n):
            if a == 2 and lo < HALF:
                t = keep.tile([P, n], I32, name=f"gw{a}_{lo}", tag=f"late{lo // N}", align_bytes=64)
            else:
                t = keep.tile([P, n], I32, name=f"gw{a}_{lo}", align_bytes=64)
            nc.vector.tensor_copy(t[:].bitcast(U32), tab_w[a][:].bitcast(U32).indirect(offs_t[:, cols(lo, n)]))
            for c in range(lo, lo + n, N):
                gw[a, c // N] = t[:, c - lo : c - lo + N].bitcast(FP8X4)

        def gather_tab2_scales():
            packed = keep.tile([P, S // 4], I32, name="g2s", align_bytes=64)
            nc.vector.tensor_copy(packed[:].bitcast(U8), tab2_s[:].bitcast(U8).indirect(offs2_t[:]))
            for b in range(U_PASSES):
                t = packed if b == 0 else moved[b - 1]
                if b > 0:
                    nc.scalar.dma_start(t[0:112, :], packed[4 * b : 4 * b + 112, :])
                for c in range(S // N):
                    g2s[b, c] = t[:].bitcast(U8)[:, N * c : N * (c + 1)]

        def gather_tab2_words(m, lo, n):
            if lo == 0:
                t = keep.tile([P, HALF], I32, name=f"pair{m}", align_bytes=64)
            else:
                t = keep.tile([P, N], I32, name=f"pair{m}_{lo}", tag="late1", align_bytes=64)
            nc.vector.tensor_copy(t[:, 0:n].bitcast(U32), tab2_w[m][:].bitcast(U32).indirect(offs2_t[:, cols(lo, n)]))
            w = keep.tile([P, 2, 2 * n], U8, name=f"g2w{m}_{lo}", align_bytes=64)
            nc.vector.tensor_copy(w[:].bitcast(U16), t[:, 0:n].bitcast(U16).rearrange("p (n h) -> p h n", h=2))
            for h in range(2):
                for c in range(lo, lo + n, N):
                    g2w[2 * m + h, c // N] = w[:, h, 2 * (c - lo) : 2 * (c - lo + N)].bitcast(FP4X4)

        u_codes = {}
        u_scales = {}

        def interleave_u(a):
            grouped = stage.tile([P, M, 4], BF16, name="grouped", align_bytes=64)
            nc.scalar.copy(grouped[:], u_raw[a].rearrange("p j n -> p n j"))
            u_codes[a] = keep.tile([P, M], U32, name=f"u_codes{a}", align_bytes=64)
            u_scales[a] = keep.tile([P, M], U8, name=f"u_scales{a}", align_bytes=64)
            return grouped

        def quantise_u(a, grouped):
            nc.vector.quantize_mx(
                out=u_codes[a][:].bitcast(FP8X4), scales=u_scales[a][:], in_=grouped[:].rearrange("p n j -> p (n j)")
            )

        acc = {}

        def banks(c):
            for m in range(4):
                acc[c, m] = psum.tile([P, N], F32, name=f"bank{c % 2}{m}")

        def multiply_tab(a, c, start, stop):
            for m in range(4):
                nc.tensor.matmul_mx(
                    out=acc[c, m][:],
                    lhsT=w4_w[:, a, 64 * m : 64 * (m + 1)].bitcast(FP4X4),
                    lhsT_scale=w4_s[:, a, 32 * m : 32 * (m + 1)].bitcast(U8),
                    rhs=gw[a, c],
                    rhs_scale=gs[a, c],
                    start=start,
                    stop=stop,
                )

        def multiply_tab2(b, c, start, stop):
            for m in range(4):
                nc.tensor.matmul_mx(
                    out=acc[c, m][:],
                    lhsT=u_codes[b][:, P * m : P * (m + 1)].bitcast(FP8X4),
                    lhsT_scale=u_scales[b][:, P * m : P * (m + 1)],
                    rhs=g2w[b, c],
                    rhs_scale=g2s[b, c],
                    start=start,
                    stop=stop,
                )

        copied = {}

        def empty_banks(c):
            for m in range(4):
                copied[c, m] = ring.tile([P, N], F32, name="o")
                nc.scalar.copy(copied[c, m][:], acc[c, m][:])

        def add_and_store(c):
            for m in range(4):
                res = r_t[c // 2][:, m, N * (c % 2) : N * (c % 2 + 1)]
                if (c, m) in copied:
                    o = copied[c, m]
                    nc.vector.tensor_tensor(o[:], o[:], res, ADD)
                else:
                    o = ring.tile([P, N], F32, name="o")
                    nc.vector.tensor_tensor(o[:], acc[c, m][:], res, ADD)
                nc.sync.dma_start(out[P * m : P * (m + 1), N * c : N * (c + 1)], o[:])

        banks(0)
        banks(1)
        gather_tab_scales(0, 0, S)
        gather_tab_words(0, 0, HALF)
        for c in (0, 1):
            multiply_tab(0, c, True, False)
        gather_tab_words(0, HALF, HALF)
        gather_tab2_scales()
        gather_tab_words(1, 0, HALF)
        gather_tab_words(1, HALF, HALF)
        load_tab_words(2)
        gather_tab_scales(1, 0, HALF)
        for c in (0, 1):
            multiply_tab(1, c, False, False)
        g0 = interleave_u(0)
        g1 = interleave_u(1)
        gather_tab2_words(0, 0, HALF)
        quantise_u(0, g0)
        quantise_u(1, g1)
        for b in (0, 1):
            for c in (0, 1):
                multiply_tab2(b, c, False, False)
        load_r(0)
        g2 = interleave_u(2)
        g3 = interleave_u(3)
        load_r(1)
        gather_tab2_words(1, 0, HALF)
        gather_tab_scales(2, 0, HALF)
        quantise_u(2, g2)
        quantise_u(3, g3)
        for b in (2, 3):
            for c in (0, 1):
                multiply_tab2(b, c, False, False)
        for c in (0, 1):
            gather_tab_words(2, N * c, N)
            multiply_tab(2, c, False, True)
            empty_banks(c)

        gather_tab_scales(1, HALF, HALF)
        gather_tab_scales(2, HALF, HALF)
        for c in (2, 3):
            banks(c)
            multiply_tab(0, c, True, False)
            multiply_tab(1, c, False, False)
        for c in (2, 3):
            lo = N * c
            for h in (0, 1):
                gather_tab2_words(h, lo, N)
                for b in (2 * h, 2 * h + 1):
                    multiply_tab2(b, c, False, False)
            gather_tab_words(2, lo, N)
            multiply_tab(2, c, False, True)
            add_and_store(c - 2)
        add_and_store(2)
        add_and_store(3)
